import numpy as np
import ml_dtypes


def mxq(x, axis, fmt="e4m3"):
    dtype, down = {"e4m3": (ml_dtypes.float8_e4m3fn, 7), "e5m2": (ml_dtypes.float8_e5m2, 14)}[fmt]
    v = np.moveaxis(np.asarray(x, np.float32).astype(ml_dtypes.bfloat16).astype(np.float64), axis, -1)
    blocks = v.reshape(v.shape[:-1] + (-1, 32))
    amax = np.abs(blocks).max(-1, keepdims=True)
    byte = np.maximum(np.where(amax > 0, np.frexp(amax)[1] - 1 + 127, 0) - down, 1)
    scale = np.exp2(byte - 127.0)
    codes = (blocks / scale).astype(np.float32).astype(dtype).astype(np.float64)
    return np.moveaxis((codes * scale).reshape(v.shape), -1, axis)


WIDE = False


def mx_kscale(k):
    if not WIDE:
        return np.ones(k)
    levels = np.array([30, -30])
    if k % 512:
        return np.exp2(np.random.permutation(np.resize(levels, k // 32))).repeat(32)
    a = np.empty((k // 512, 16))
    for p in range(k // 512):
        a[p, :8] = np.random.permutation(np.resize(levels, 8))
        for g in range(8):
            far = levels[np.abs(levels - a[p, g]) >= 10]
            a[p, g + 8] = far[np.random.randint(len(far))]
    return np.exp2(a.ravel()).repeat(32)


def f64(x):
    return np.asarray(x).astype(np.float64)


def striped(idx):
    return np.tile(np.asarray(idx).reshape(-1, 16).T, (8, 1)).astype(np.uint16)


def unstriped(offs):
    return offs[:16].T.reshape(-1).astype(np.int64)


E2M1 = np.array([0.0, 0.5, 1.0, 1.5, 2.0, 3.0, 4.0, 6.0, -0.0, -0.5, -1.0, -1.5, -2.0, -3.0, -4.0, -6.0])


def pack_weight(w, fmt):
    k, n = w.shape
    w = f64(np.asarray(w, np.float32).astype(ml_dtypes.bfloat16)).reshape(k // 32, 32, n)
    amax = np.abs(w).max(1)
    if fmt in ("e4m3", "e5m2"):
        byte = np.frexp(amax)[1] - 1 + 127 - (7 if fmt == "e4m3" else 14)
    else:
        mant, ex = np.frexp(amax / 6.0)
        byte = np.where(mant > 0.5, ex, ex - 1) + 127
    byte = np.clip(np.where(amax > 0, byte, 1), 1, 254)
    scaled = (w * np.exp2(127.0 - byte)[:, None, :]).reshape(k, n).astype(np.float32)
    by_word = np.ascontiguousarray(scaled.reshape(k // 512, 128, 4, n).transpose(0, 1, 3, 2))
    if fmt in ("e4m3", "e5m2"):
        words = by_word.astype(ml_dtypes.float8_e4m3fn if fmt == "e4m3" else ml_dtypes.float8_e5m2).view(np.uint8)
    else:
        c = by_word.astype(ml_dtypes.float4_e2m1fn).view(np.uint8) & 0xF
        words = (c[..., 0::2] | (c[..., 1::2] << 4)).reshape(k // 512, 128, 2 * n)
    return np.ascontiguousarray(words), np.ascontiguousarray(byte.astype(np.uint8).reshape(k // 512, 16, n))


def unpack_weight(words, scales, fmt):
    g, _, n = scales.shape
    words = np.ascontiguousarray(words).reshape(g, 128, n, -1)
    if fmt in ("e4m3", "e5m2"):
        vals = words.view(ml_dtypes.float8_e4m3fn if fmt == "e4m3" else ml_dtypes.float8_e5m2).astype(np.float64)
    else:
        nib = np.empty((g, 128, n, 4), np.uint8)
        nib[..., 0::2] = words & 0xF
        nib[..., 1::2] = words >> 4
        vals = E2M1[nib]
    vals = vals * np.repeat(np.exp2(scales.astype(np.float64) - 127.0), 8, axis=1)[..., None]
    return vals.transpose(0, 1, 3, 2).reshape(g * 512, n)


def e4m3fn_bytes(y):
    return np.clip(np.asarray(y, np.float64), -448.0, 448.0).astype(np.float32).astype(ml_dtypes.float8_e4m3fn).view(np.uint8)


def e4m3fn_values(b):
    return np.asarray(b, np.uint8).view(ml_dtypes.float8_e4m3fn).astype(np.float64)


def sgn(shape):
    return np.random.uniform(0.5, 2.0, shape) * np.where(np.random.standard_normal(shape) < 0, -1.0, 1.0)


K, T, J, R, C, V, I, O, N = 512, 1024, 256, 512, 512, 512, 128, 256, 256


def setup_inputs():
    n = np.random.standard_normal
    idx = np.random.permutation(T)[:J]
    idx2 = np.random.permutation(J)[:I]
    idx3 = np.random.permutation(V)[:I]
    idx4 = np.random.permutation(C)[:I]
    idx5 = np.random.permutation(C)[:O]
    fk = mx_kscale(K)
    fr = mx_kscale(R)
    xtp = pack_weight(n((K, T)) / fk[:, None], "e4m3")
    wp = pack_weight(n((K, R)) * 1 / np.sqrt(K) * fk[:, None], "e2m1")
    wbp = pack_weight(n((R, N)) * 1 / np.sqrt(R) / fr[:, None], "e5m2")
    return {
        "xt_words": xtp[0],
        "xt_scales": xtp[1],
        "w_words": wp[0],
        "w_scales": wp[1],
        "ca": e4m3fn_bytes(60.0 * n((R, V))),
        "st": (np.random.uniform(0.004, 0.012, (R, 1)) * fr[:, None]).astype(np.float32),
        "sa": (sgn((R, 1))).astype(np.float32),
        "wb_words": wbp[0],
        "wb_scales": wbp[1],
        "offs": striped(idx),
        "offs2": striped(idx2),
        "offs3": striped(idx3),
        "offs4": striped(idx4),
        "offs5": striped(idx5),
    }


def reference(xt_words, xt_scales, w_words, w_scales, ca, st, sa, wb_words, wb_scales, offs, offs2, offs3, offs4, offs5):
    idx = unstriped(offs)
    idx2 = unstriped(offs2)
    idx3 = unstriped(offs3)
    idx4 = unstriped(offs4)
    idx5 = unstriped(offs5)
    xtu = unpack_weight(xt_words, xt_scales, "e4m3")
    wu = unpack_weight(w_words, w_scales, "e2m1")
    wbu = unpack_weight(wb_words, wb_scales, "e5m2")
    xtidxg = xtu[:, idx]
    a = wu.T @ xtidxg
    g1 = e4m3fn_values(ca)[:, idx3] * f64(st)
    h1 = a[:, idx2] * g1
    pw = np.zeros((R, C))
    pw[:, idx4] = h1 * f64(sa)
    hid = pw[:, idx5]
    hidq = mxq(hid, 0, "e4m3")
    p = wbu.T @ hidq
    return p

@@ -1,0 +1,168 @@
+from contextlib import ExitStack
+
+import concourse.mybir as mybir
+
+K, T, J, R, C, V, I, O, N = 512, 1024, 256, 512, 512, 512, 128, 256, 256
+FLOPS = 2 * K * R * J + 2 * R * N * O
+
+F32 = mybir.dt.float32
+BF16 = mybir.dt.bfloat16
+I32 = mybir.dt.int32
+U32 = mybir.dt.uint32
+U16 = mybir.dt.uint16
+U8 = mybir.dt.uint8
+E4M3 = mybir.dt.float8_e4m3fn
+E4M3X4 = mybir.dt.float8_e4m3fn_x4
+E5M2X4 = mybir.dt.float8_e5m2_x4
+E2M1X4 = mybir.dt.float4_e2m1fn_x4
+COPY = mybir.ActivationFunctionType.Copy
+MULT = mybir.AluOpType.mult
+
+P = 128
+PACK = 4
+HALF = O // 2
+
+
+def tile_list_relayed_kernel(tc, xt_words, xt_scales, w_words, w_scales, ca, st, sa, wb_words, wb_scales,
+                                offs, offs2, offs3, offs4, offs5, out):
+    nc = tc.nc
+    with ExitStack() as ctx:
+        sb = ctx.enter_context(tc.tile_pool(name="sb", bufs=1))
+        ps = ctx.enter_context(tc.psum_pool(name="ps", bufs=1))
+
+        def tiles(name, shape, dtype, count=PACK):
+            return [sb.tile(shape, dtype, name="%s%d" % (name, t), align_bytes=64) for t in range(count)]
+
+        tok_list = sb.tile([P, J // 16], U16, name="tok_list")
+        slot_list = sb.tile([P, I // 16], U16, name="slot_list")
+        gate_list = sb.tile([P, I // 16], U16, name="gate_list")
+        put_list = sb.tile([P, I // 16], U16, name="put_list")
+        take_list = sb.tile([P, O // 16], U16, name="take_list")
+        x_words = sb.tile([P, T], U32, name="x_words", align_bytes=64)
+        x_plane = sb.tile([P, T], U8, name="x_plane", align_bytes=64)
+        w_raw = sb.tile([P, R], U16, name="w_raw", align_bytes=64)
+        w_plane = sb.tile([P, R], U8, name="w_plane", align_bytes=64)
+        wb_codes = sb.tile([P, N], U32, name="wb_codes", align_bytes=64)
+        wb_plane = sb.tile([P, N], U8, name="wb_plane", align_bytes=64)
+        st_sb = sb.tile([P, PACK], F32, name="st_sb")
+        sa_sb = sb.tile([P, PACK], F32, name="sa_sb")
+        gates = tiles("gates", [P, V], U8)
+        board = tiles("board", [P, C], F32)
+
+        def load_plane(eng, plane, rows, q):
+            four = rows[0, 4 * q : 4 * q + 4, :].bitcast(I32)
+            eng.dma_start(out=plane[32 * q : 32 * q + 32, :].bitcast(I32),
+                          in_=four.unsqueeze(0).to_broadcast([8, 4, four.shape[1]]))
+
+        ca_rows = ca.rearrange("(p t) v -> t p v", t=PACK)
+        nc.sync.dma_start(tok_list[:], offs)
+        load_plane(nc.scalar, x_plane, xt_scales, 0)
+        load_plane(nc.sync, x_plane, xt_scales, 1)
+        load_plane(nc.scalar, x_plane, xt_scales, 2)
+        load_plane(nc.sync, x_plane, xt_scales, 3)
+        nc.scalar.dma_start(out=w_raw[:].bitcast(I32), in_=w_words[0].bitcast(I32))
+        nc.sync.dma_start(out=x_words[:].bitcast(I32), in_=xt_words[0].rearrange("p n t -> p (n t)").bitcast(I32))
+        load_plane(nc.scalar, w_plane, w_scales, 0)
+        load_plane(nc.sync, w_plane, w_scales, 1)
+        load_plane(nc.sync, w_plane, w_scales, 2)
+        load_plane(nc.sync, w_plane, w_scales, 3)
+        nc.gpsimd.dma_start(out=st_sb[:], in_=st.rearrange("(p t) o -> p (t o)", t=PACK))
+        nc.gpsimd.dma_start(out=sa_sb[:], in_=sa.rearrange("(p t) o -> p (t o)", t=PACK))
+        nc.sync.dma_start(gate_list[:], offs3)
+        nc.sync.dma_start(out=gates[0][:], in_=ca_rows[0])
+        nc.sync.dma_start(slot_list[:], offs2)
+        nc.sync.dma_start(out=gates[1][:], in_=ca_rows[1])
+        nc.sync.dma_start(put_list[:], offs4)
+        nc.sync.dma_start(take_list[:], offs5)
+        nc.sync.dma_start(out=gates[2][:], in_=ca_rows[2])
+        nc.sync.dma_start(out=gates[3][:], in_=ca_rows[3])
+        nc.sync.dma_start(out=wb_codes[:].bitcast(I32), in_=wb_words[0].rearrange("p n t -> p (n t)").bitcast(I32))
+        load_plane(nc.sync, wb_plane, wb_scales, 0)
+        load_plane(nc.sync, wb_plane, wb_scales, 1)
+        load_plane(nc.sync, wb_plane, wb_scales, 2)
+        load_plane(nc.sync, wb_plane, wb_scales, 3)
+        for t in range(PACK):
+            nc.vector.memset(board[t][:], 0.0)
+
+        xg_plane = sb.tile([P, J], U8, name="xg_plane", align_bytes=64)
+        xg_words = sb.tile([P, J], U32, name="xg_words", align_bytes=64)
+        w_codes = sb.tile([P, PACK, P], U16, name="w_codes", align_bytes=64)
+        w_first = sb.tile([P, P], U8, name="w_first", align_bytes=64)
+        w_rest = sb.tile([P, PACK - 1, P], U8, name="w_rest", align_bytes=64)
+        w_dealt = [w_first[:]] + [w_rest[:, t, :] for t in range(PACK - 1)]
+        nc.vector.tensor_copy(out=xg_plane[:], in_=x_plane[:].indirect(tok_list[:]))
+        nc.vector.tensor_copy(out=w_codes[:], in_=w_raw[:].rearrange("p (q t) -> p t q", t=PACK))
+        nc.vector.tensor_copy(out=xg_words[:], in_=x_words[:].indirect(tok_list[:]))
+        nc.vector.tensor_copy(out=w_first[:], in_=w_plane[:, 0:R:PACK])
+        nc.vector.tensor_copy(out=w_rest[:], in_=w_plane[:].rearrange("p (q t) -> p t q", t=PACK)[:, 1:PACK, :])
+
+        a_ps = [ps.tile([P, J], F32, name="a_ps%d" % t) for t in range(PACK)]
+        a_sb = tiles("a_sb", [P, J], F32)
+        gate_bytes = tiles("gate_bytes", [P, I], U8)
+        g1 = tiles("g1", [P, I], F32)
+        h1 = tiles("h1", [P, I], F32)
+        hid = sb.tile([P, PACK * O], BF16, name="hid", align_bytes=64)
+
+        def first_product(t):
+            nc.tensor.matmul_mx(out=a_ps[t][:], lhsT=w_codes[:, t, :].bitcast(E2M1X4), lhsT_scale=w_dealt[t],
+                                rhs=xg_words[:].bitcast(E4M3X4), rhs_scale=xg_plane[:], start=True, stop=True)
+
+        def gate(t):
+            nc.vector.tensor_copy(out=gate_bytes[t][:], in_=gates[t][:].indirect(gate_list[:]))
+            nc.vector.tensor_scalar(out=g1[t][:], in0=gate_bytes[t][:].bitcast(E4M3), scalar1=st_sb[:, t : t + 1],
+                                    scalar2=None, op0=MULT)
+
+        def evacuate(t):
+            if t < 2:
+                nc.scalar.activation(out=a_sb[t][:], in_=a_ps[t][:], func=COPY)
+            else:
+                nc.vector.tensor_copy(out=a_sb[t][:], in_=a_ps[t][:])
+
+        def seat(t):
+            nc.vector.tensor_tensor(out=h1[t][:], in0=a_sb[t][:].indirect(slot_list[:]), in1=g1[t][:], op=MULT)
+
+        def put(t):
+            nc.scalar.activation(out=board[t][:].indirect(put_list[:]), in_=h1[t][:], func=COPY, scale=sa_sb[:, t : t + 1])
+
+        def take(t, first, count):
+            nc.scalar.activation(out=hid[:, PACK * first + t : PACK * (first + count) : PACK],
+                                 in_=board[t][:].indirect(take_list[:, first // 16 : (first + count) // 16]), func=COPY)
+
+        for t in range(PACK):
+            first_product(t)
+        evacuate(0)
+        evacuate(1)
+        gate(0)
+        gate(1)
+        seat(0)
+        put(0)
+        seat(1)
+        put(1)
+        for t in range(2, PACK):
+            evacuate(t)
+            gate(t)
+            take(t - 2, 0, O)
+            seat(t)
+            put(t)
+        for h in range(2):
+            take(PACK - 2, h * HALF, HALF)
+
+        out_rows = out.rearrange("(m p) o -> m p o", p=P)
+        for h in range(2):
+            take(PACK - 1, h * HALF, HALF)
+            codes = sb.tile([P, HALF], U32, name="codes%d" % h, align_bytes=64)
+            plane = sb.tile([P, HALF], U8, name="plane%d" % h, align_bytes=64)
+            nc.vector.quantize_mx(out=codes[:].bitcast(E4M3X4), scales=plane[:],
+                                  in_=hid[:, PACK * HALF * h : PACK * HALF * (h + 1)])
+            for m in range(N // P):
+                acc = ps.tile([P, HALF], F32, name="acc%d%d" % (h, m))
+                cols = slice(m * P, (m + 1) * P)
+                nc.tensor.matmul_mx(out=acc[:], lhsT=wb_codes[:, cols].bitcast(E5M2X4), lhsT_scale=wb_plane[:, cols],
+                                    rhs=codes[:].bitcast(E4M3X4), rhs_scale=plane[:], start=True, stop=True)
+                res = sb.tile([P, HALF], F32, name="res%d%d" % (h, m))
+                if h == 1 and m == 1:
+                    nc.scalar.copy(out=res[:], in_=acc[:])
+                    nc.scalar.dma_start(out=out_rows[m, :, h * HALF : (h + 1) * HALF], in_=res[:])
+                else:
+                    nc.vector.tensor_copy(out=res[:], in_=acc[:])
+                    nc.sync.dma_start(out=out_rows[m, :, h * HALF : (h + 1) * HALF], in_=res[:])

@@ -61,8 +61,8 @@ def tile_list_relayed_kernel(tc, xt_words, xt_scales, w_words, w_scales, ca, st,
         load_plane(nc.scalar, x_plane, xt_scales, 2)
         load_plane(nc.sync, x_plane, xt_scales, 3)
         nc.scalar.dma_start(out=w_raw[:].bitcast(I32), in_=w_words[0].bitcast(I32))
-        nc.sync.dma_start(out=x_words[:].bitcast(I32), in_=xt_words[0].rearrange("p n t -> p (n t)").bitcast(I32))
-        load_plane(nc.scalar, w_plane, w_scales, 0)
+        load_plane(nc.sync, w_plane, w_scales, 0)
+        nc.scalar.dma_start(out=x_words[:].bitcast(I32), in_=xt_words[0].rearrange("p n t -> p (n t)").bitcast(I32))
         load_plane(nc.sync, w_plane, w_scales, 1)
         load_plane(nc.sync, w_plane, w_scales, 2)
         load_plane(nc.sync, w_plane, w_scales, 3)
@@ -97,22 +97,26 @@ def tile_list_relayed_kernel(tc, xt_words, xt_scales, w_words, w_scales, ca, st,
         nc.vector.tensor_copy(out=w_rest[:], in_=w_plane[:].rearrange("p (q t) -> p t q", t=PACK)[:, 1:PACK, :])
 
         a_ps = [ps.tile([P, J], F32, name="a_ps%d" % t) for t in range(PACK)]
-        a_sb = tiles("a_sb", [P, J], F32)
-        gate_bytes = tiles("gate_bytes", [P, I], U8)
-        g1 = tiles("g1", [P, I], F32)
+        a_sb = {}
+        g1 = {}
+        hid = {}
+        bytes_tag = ["bytes0", "bytes1", "slot0", "slot0"]
+        g1_tag = ["slot0", "slot1", "g2", "slot2"]
         h1 = tiles("h1", [P, I], F32)
-        hid = sb.tile([P, PACK * O], BF16, name="hid", align_bytes=64)
 
         def first_product(t):
             nc.tensor.matmul_mx(out=a_ps[t][:], lhsT=w_codes[:, t, :].bitcast(E2M1X4), lhsT_scale=w_dealt[t],
                                 rhs=xg_words[:].bitcast(E4M3X4), rhs_scale=xg_plane[:], start=True, stop=True)
 
         def gate(t):
-            nc.vector.tensor_copy(out=gate_bytes[t][:], in_=gates[t][:].indirect(gate_list[:]))
-            nc.vector.tensor_scalar(out=g1[t][:], in0=gate_bytes[t][:].bitcast(E4M3), scalar1=st_sb[:, t : t + 1],
+            gate_bytes = sb.tile([P, I], U8, name="gate_bytes%d" % t, tag=bytes_tag[t], align_bytes=64)
+            g1[t] = sb.tile([P, I], F32, name="g1_%d" % t, tag=g1_tag[t], align_bytes=64)
+            nc.vector.tensor_copy(out=gate_bytes[:], in_=gates[t][:].indirect(gate_list[:]))
+            nc.vector.tensor_scalar(out=g1[t][:], in0=gate_bytes[:].bitcast(E4M3), scalar1=st_sb[:, t : t + 1],
                                     scalar2=None, op0=MULT)
 
         def evacuate(t):
+            a_sb[t] = sb.tile([P, J], F32, name="a_sb%d" % t, tag="a%d" % (t % 2))
             if t < 2:
                 nc.scalar.activation(out=a_sb[t][:], in_=a_ps[t][:], func=COPY)
             else:
@@ -124,45 +128,70 @@ def tile_list_relayed_kernel(tc, xt_words, xt_scales, w_words, w_scales, ca, st,
         def put(t):
             nc.scalar.activation(out=board[t][:].indirect(put_list[:]), in_=h1[t][:], func=COPY, scale=sa_sb[:, t : t + 1])
 
-        def take(t, first, count):
-            nc.scalar.activation(out=hid[:, PACK * first + t : PACK * (first + count) : PACK],
-                                 in_=board[t][:].indirect(take_list[:, first // 16 : (first + count) // 16]), func=COPY)
+        def open_half(h):
+            hid[h] = sb.tile([P, PACK * HALF], BF16, name="hid%d" % h, tag="slot%d" % (h + 1), align_bytes=64)
+
+        def take(t, h):
+            nc.scalar.activation(out=hid[h][:, t : PACK * HALF : PACK],
+                                 in_=board[t][:].indirect(take_list[:, h * HALF // 16 : (h + 1) * HALF // 16]), func=COPY)
+
+        def finish(h):
+            codes = sb.tile([P, HALF], U32, name="codes%d" % h, align_bytes=64)
+            plane = sb.tile([P, HALF], U8, name="plane%d" % h, align_bytes=64)
+            nc.vector.quantize_mx(out=codes[:].bitcast(E4M3X4), scales=plane[:], in_=hid[h][:])
+
+            def product(acc, m):
+                cols = slice(m * P, (m + 1) * P)
+                nc.tensor.matmul_mx(out=acc, lhsT=wb_codes[:, cols].bitcast(E5M2X4), lhsT_scale=wb_plane[:, cols],
+                                    rhs=codes[:].bitcast(E4M3X4), rhs_scale=plane[:], start=True, stop=True)
+
+            places = slice(h * HALF, (h + 1) * HALF)
+            if h == 0:
+                acc = ps.tile([P, 2, HALF], F32, name="acc_both")
+                res = sb.tile([P, 2, HALF], F32, name="res_both")
+                product(acc[:, 0, :], 0)
+                product(acc[:, 1, :], 1)
+                nc.vector.tensor_copy(out=res[:], in_=acc[:])
+                nc.sync.dma_start(out=out.rearrange("(m p) o -> p m o", p=P)[:, :, places], in_=res[:])
+            else:
+                acc0 = ps.tile([P, HALF], F32, name="acc0")
+                acc1 = ps.tile([P, HALF], F32, name="acc1")
+                res0 = sb.tile([P, HALF], F32, name="res0")
+                res1 = sb.tile([P, HALF], F32, name="res1")
+                product(acc0[:], 0)
+                product(acc1[:], 1)
+                nc.vector.tensor_copy(out=res0[:], in_=acc0[:])
+                nc.sync.dma_start(out=out[0:P, places], in_=res0[:])
+                nc.scalar.copy(out=res1[:], in_=acc1[:])
+                nc.scalar.dma_start(out=out[P : 2 * P, places], in_=res1[:])
 
         for t in range(PACK):
             first_product(t)
         evacuate(0)
         evacuate(1)
         gate(0)
-        gate(1)
         seat(0)
         put(0)
+        gate(1)
         seat(1)
         put(1)
-        for t in range(2, PACK):
-            evacuate(t)
-            gate(t)
-            take(t - 2, 0, O)
-            seat(t)
-            put(t)
-        for h in range(2):
-            take(PACK - 2, h * HALF, HALF)
-
-        out_rows = out.rearrange("(m p) o -> m p o", p=P)
-        for h in range(2):
-            take(PACK - 1, h * HALF, HALF)
-            codes = sb.tile([P, HALF], U32, name="codes%d" % h, align_bytes=64)
-            plane = sb.tile([P, HALF], U8, name="plane%d" % h, align_bytes=64)
-            nc.vector.quantize_mx(out=codes[:].bitcast(E4M3X4), scales=plane[:],
-                                  in_=hid[:, PACK * HALF * h : PACK * HALF * (h + 1)])
-            for m in range(N // P):
-                acc = ps.tile([P, HALF], F32, name="acc%d%d" % (h, m))
-                cols = slice(m * P, (m + 1) * P)
-                nc.tensor.matmul_mx(out=acc[:], lhsT=wb_codes[:, cols].bitcast(E5M2X4), lhsT_scale=wb_plane[:, cols],
-                                    rhs=codes[:].bitcast(E4M3X4), rhs_scale=plane[:], start=True, stop=True)
-                res = sb.tile([P, HALF], F32, name="res%d%d" % (h, m))
-                if h == 1 and m == 1:
-                    nc.scalar.copy(out=res[:], in_=acc[:])
-                    nc.scalar.dma_start(out=out_rows[m, :, h * HALF : (h + 1) * HALF], in_=res[:])
-                else:
-                    nc.vector.tensor_copy(out=res[:], in_=acc[:])
-                    nc.sync.dma_start(out=out_rows[m, :, h * HALF : (h + 1) * HALF], in_=res[:])
+        open_half(0)
+        gate(2)
+        evacuate(2)
+        seat(2)
+        put(2)
+        take(0, 0)
+        take(1, 0)
+        gate(3)
+        evacuate(3)
+        seat(3)
+        put(3)
+        take(2, 0)
+        open_half(1)
+        take(0, 1)
+        take(3, 0)
+        finish(0)
+        take(1, 1)
+        take(2, 1)
+        take(3, 1)
+        finish(1)

from contextlib import ExitStack

import concourse.mybir as mybir

K, T, J, R, C, V, I, O, N = 512, 1024, 256, 512, 512, 512, 128, 256, 256
FLOPS = 2 * K * R * J + 2 * R * N * O

F32 = mybir.dt.float32
BF16 = mybir.dt.bfloat16
I32 = mybir.dt.int32
U32 = mybir.dt.uint32
U16 = mybir.dt.uint16
U8 = mybir.dt.uint8
E4M3 = mybir.dt.float8_e4m3fn
E4M3X4 = mybir.dt.float8_e4m3fn_x4
E5M2X4 = mybir.dt.float8_e5m2_x4
E2M1X4 = mybir.dt.float4_e2m1fn_x4
COPY = mybir.ActivationFunctionType.Copy
MULT = mybir.AluOpType.mult

P = 128
PACK = 4
HALF = O // 2


def tile_list_relayed_kernel(tc, xt_words, xt_scales, w_words, w_scales, ca, st, sa, wb_words, wb_scales,
                                offs, offs2, offs3, offs4, offs5, out):
    nc = tc.nc
    with ExitStack() as ctx:
        sb = ctx.enter_context(tc.tile_pool(name="sb", bufs=1))
        ps = ctx.enter_context(tc.psum_pool(name="ps", bufs=1))

        def tiles(name, shape, dtype, count=PACK):
            return [sb.tile(shape, dtype, name="%s%d" % (name, t), align_bytes=64) for t in range(count)]

        tok_list = sb.tile([P, J // 16], U16, name="tok_list")
        slot_list = sb.tile([P, I // 16], U16, name="slot_list")
        gate_list = sb.tile([P, I // 16], U16, name="gate_list")
        put_list = sb.tile([P, I // 16], U16, name="put_list")
        take_list = sb.tile([P, O // 16], U16, name="take_list")
        x_words = sb.tile([P, T], U32, name="x_words", align_bytes=64)
        x_plane = sb.tile([P, T], U8, name="x_plane", align_bytes=64)
        w_raw = sb.tile([P, R], U16, name="w_raw", align_bytes=64)
        w_plane = sb.tile([P, R], U8, name="w_plane", align_bytes=64)
        wb_codes = sb.tile([P, N], U32, name="wb_codes", align_bytes=64)
        wb_plane = sb.tile([P, N], U8, name="wb_plane", align_bytes=64)
        st_sb = sb.tile([P, PACK], F32, name="st_sb")
        sa_sb = sb.tile([P, PACK], F32, name="sa_sb")
        gates = tiles("gates", [P, V], U8)
        board = tiles("board", [P, C], F32)

        def load_plane(eng, plane, rows, q):
            four = rows[0, 4 * q : 4 * q + 4, :].bitcast(I32)
            eng.dma_start(out=plane[32 * q : 32 * q + 32, :].bitcast(I32),
                          in_=four.unsqueeze(0).to_broadcast([8, 4, four.shape[1]]))

        ca_rows = ca.rearrange("(p t) v -> t p v", t=PACK)
        nc.sync.dma_start(tok_list[:], offs)
        load_plane(nc.scalar, x_plane, xt_scales, 0)
        load_plane(nc.sync, x_plane, xt_scales, 1)
        load_plane(nc.scalar, x_plane, xt_scales, 2)
        load_plane(nc.sync, x_plane, xt_scales, 3)
        nc.scalar.dma_start(out=w_raw[:].bitcast(I32), in_=w_words[0].bitcast(I32))
        load_plane(nc.sync, w_plane, w_scales, 0)
        nc.scalar.dma_start(out=x_words[:].bitcast(I32), in_=xt_words[0].rearrange("p n t -> p (n t)").bitcast(I32))
        load_plane(nc.sync, w_plane, w_scales, 1)
        load_plane(nc.sync, w_plane, w_scales, 2)
        load_plane(nc.sync, w_plane, w_scales, 3)
        nc.gpsimd.dma_start(out=st_sb[:], in_=st.rearrange("(p t) o -> p (t o)", t=PACK))
        nc.gpsimd.dma_start(out=sa_sb[:], in_=sa.rearrange("(p t) o -> p (t o)", t=PACK))
        nc.sync.dma_start(gate_list[:], offs3)
        nc.sync.dma_start(out=gates[0][:], in_=ca_rows[0])
        nc.sync.dma_start(slot_list[:], offs2)
        nc.sync.dma_start(out=gates[1][:], in_=ca_rows[1])
        nc.sync.dma_start(put_list[:], offs4)
        nc.sync.dma_start(take_list[:], offs5)
        nc.sync.dma_start(out=gates[2][:], in_=ca_rows[2])
        nc.sync.dma_start(out=gates[3][:], in_=ca_rows[3])
        nc.sync.dma_start(out=wb_codes[:].bitcast(I32), in_=wb_words[0].rearrange("p n t -> p (n t)").bitcast(I32))
        load_plane(nc.sync, wb_plane, wb_scales, 0)
        load_plane(nc.sync, wb_plane, wb_scales, 1)
        load_plane(nc.sync, wb_plane, wb_scales, 2)
        load_plane(nc.sync, wb_plane, wb_scales, 3)
        for t in range(PACK):
            nc.vector.memset(board[t][:], 0.0)

        xg_plane = sb.tile([P, J], U8, name="xg_plane", align_bytes=64)
        xg_words = sb.tile([P, J], U32, name="xg_words", align_bytes=64)
        w_codes = sb.tile([P, PACK, P], U16, name="w_codes", align_bytes=64)
        w_first = sb.tile([P, P], U8, name="w_first", align_bytes=64)
        w_rest = sb.tile([P, PACK - 1, P], U8, name="w_rest", align_bytes=64)
        w_dealt = [w_first[:]] + [w_rest[:, t, :] for t in range(PACK - 1)]
        nc.vector.tensor_copy(out=xg_plane[:], in_=x_plane[:].indirect(tok_list[:]))
        nc.vector.tensor_copy(out=w_codes[:], in_=w_raw[:].rearrange("p (q t) -> p t q", t=PACK))
        nc.vector.tensor_copy(out=xg_words[:], in_=x_words[:].indirect(tok_list[:]))
        nc.vector.tensor_copy(out=w_first[:], in_=w_plane[:, 0:R:PACK])
        nc.vector.tensor_copy(out=w_rest[:], in_=w_plane[:].rearrange("p (q t) -> p t q", t=PACK)[:, 1:PACK, :])

        a_ps = [ps.tile([P, J], F32, name="a_ps%d" % t) for t in range(PACK)]
        a_sb = {}
        g1 = {}
        hid = {}
        bytes_tag = ["bytes0", "bytes1", "slot0", "slot0"]
        g1_tag = ["slot0", "slot1", "g2", "slot2"]
        h1 = tiles("h1", [P, I], F32)

        def first_product(t):
            nc.tensor.matmul_mx(out=a_ps[t][:], lhsT=w_codes[:, t, :].bitcast(E2M1X4), lhsT_scale=w_dealt[t],
                                rhs=xg_words[:].bitcast(E4M3X4), rhs_scale=xg_plane[:], start=True, stop=True)

        def gate(t):
            gate_bytes = sb.tile([P, I], U8, name="gate_bytes%d" % t, tag=bytes_tag[t], align_bytes=64)
            g1[t] = sb.tile([P, I], F32, name="g1_%d" % t, tag=g1_tag[t], align_bytes=64)
            nc.vector.tensor_copy(out=gate_bytes[:], in_=gates[t][:].indirect(gate_list[:]))
            nc.vector.tensor_scalar(out=g1[t][:], in0=gate_bytes[:].bitcast(E4M3), scalar1=st_sb[:, t : t + 1],
                                    scalar2=None, op0=MULT)

        def evacuate(t):
            a_sb[t] = sb.tile([P, J], F32, name="a_sb%d" % t, tag="a%d" % (t % 2))
            if t < 2:
                nc.scalar.activation(out=a_sb[t][:], in_=a_ps[t][:], func=COPY)
            else:
                nc.vector.tensor_copy(out=a_sb[t][:], in_=a_ps[t][:])

        def seat(t):
            nc.vector.tensor_tensor(out=h1[t][:], in0=a_sb[t][:].indirect(slot_list[:]), in1=g1[t][:], op=MULT)

        def put(t):
            nc.scalar.activation(out=board[t][:].indirect(put_list[:]), in_=h1[t][:], func=COPY, scale=sa_sb[:, t : t + 1])

        def open_half(h):
            hid[h] = sb.tile([P, PACK * HALF], BF16, name="hid%d" % h, tag="slot%d" % (h + 1), align_bytes=64)

        def take(t, h):
            nc.scalar.activation(out=hid[h][:, t : PACK * HALF : PACK],
                                 in_=board[t][:].indirect(take_list[:, h * HALF // 16 : (h + 1) * HALF // 16]), func=COPY)

        def finish(h):
            codes = sb.tile([P, HALF], U32, name="codes%d" % h, align_bytes=64)
            plane = sb.tile([P, HALF], U8, name="plane%d" % h, align_bytes=64)
            nc.vector.quantize_mx(out=codes[:].bitcast(E4M3X4), scales=plane[:], in_=hid[h][:])

            def product(acc, m):
                cols = slice(m * P, (m + 1) * P)
                nc.tensor.matmul_mx(out=acc, lhsT=wb_codes[:, cols].bitcast(E5M2X4), lhsT_scale=wb_plane[:, cols],
                                    rhs=codes[:].bitcast(E4M3X4), rhs_scale=plane[:], start=True, stop=True)

            places = slice(h * HALF, (h + 1) * HALF)
            if h == 0:
                acc = ps.tile([P, 2, HALF], F32, name="acc_both")
                res = sb.tile([P, 2, HALF], F32, name="res_both")
                product(acc[:, 0, :], 0)
                product(acc[:, 1, :], 1)
                nc.vector.tensor_copy(out=res[:], in_=acc[:])
                nc.sync.dma_start(out=out.rearrange("(m p) o -> p m o", p=P)[:, :, places], in_=res[:])
            else:
                acc0 = ps.tile([P, HALF], F32, name="acc0")
                acc1 = ps.tile([P, HALF], F32, name="acc1")
                res0 = sb.tile([P, HALF], F32, name="res0")
                res1 = sb.tile([P, HALF], F32, name="res1")
                product(acc0[:], 0)
                product(acc1[:], 1)
                nc.vector.tensor_copy(out=res0[:], in_=acc0[:])
                nc.sync.dma_start(out=out[0:P, places], in_=res0[:])
                nc.scalar.copy(out=res1[:], in_=acc1[:])
                nc.scalar.dma_start(out=out[P : 2 * P, places], in_=res1[:])

        for t in range(PACK):
            first_product(t)
        evacuate(0)
        evacuate(1)
        gate(0)
        seat(0)
        put(0)
        gate(1)
        seat(1)
        put(1)
        open_half(0)
        gate(2)
        evacuate(2)
        seat(2)
        put(2)
        take(0, 0)
        take(1, 0)
        gate(3)
        evacuate(3)
        seat(3)
        put(3)
        take(2, 0)
        open_half(1)
        take(0, 1)
        take(3, 0)
        finish(0)
        take(1, 1)
        take(2, 1)
        take(3, 1)
        finish(1)
